import numpy as np
import ml_dtypes

BF16 = ml_dtypes.bfloat16


def bf(x):
    return np.asarray(x, np.float32).astype(BF16)


def f32(x):
    return np.asarray(x, np.float32)


def f64(x):
    return np.asarray(x).astype(np.float64)


def striped(idx):
    return np.tile(idx.reshape(-1, 16).T, (8, 1))


S, K, M, N, E, Q = 512, 512, 256, 512, 2, 256


def setup_inputs():
    return {"base": bf(np.random.standard_normal((M, S))), "x": bf(np.random.standard_normal((K, N))), "w": bf(np.random.standard_normal((E, K, M)) / np.sqrt(K)), "b": f32(0.5 * np.random.standard_normal((M, 1))), "offs": striped(np.random.permutation(S))}


def reference(base, x, w, b, offs):
    idx = offs[:16].T.reshape(-1)
    z = f64(base).copy()
    for e in range(E):
        z[:, idx[e * Q : (e + 1) * Q]] += f64(w)[e].T @ f64(x)[:, e * Q : (e + 1) * Q]
    return z + f64(b)

@@ -1,0 +1,55 @@
+import concourse.mybir as mybir
+from concourse.masks import make_identity
+
+BF16, F32, U16 = mybir.dt.bfloat16, mybir.dt.float32, mybir.dt.uint16
+
+P = 128
+K, N = 512, 512
+M, E = 256, 2
+Q = N // E
+KB, MB = K // P, M // P
+
+FLOPS = 2 * K * N * M
+
+
+def tile_scatter_matmul_kernel(tc, base, x, w, b, offs, out):
+    nc = tc.nc
+    with (
+        tc.tile_pool(name="held", bufs=1) as held,
+        tc.psum_pool(name="psum", bufs=1) as psum,
+    ):
+        ident = held.tile([P, P], BF16, name="ident")
+        base_t = held.tile([P, MB, N], BF16, name="base_t")
+        offs_t = held.tile([P, N // 16], U16, name="offs_t")
+        x_t = held.tile([P, KB, N], BF16, name="x_t")
+        w_t = [held.tile([P, KB, M], BF16, name=f"w_t{e}") for e in range(E)]
+        bias_t = held.tile([P, MB], F32, name="bias_t")
+        windows = [psum.tile([P, N], F32, name=f"window{m}") for m in range(MB)]
+
+        nc.sync.dma_start(base_t[:], base.rearrange("(m p) t -> p m t", p=P))
+        nc.sync.dma_start(offs_t[:], offs)
+        nc.sync.dma_start(w_t[0][:], w[0].rearrange("(p c) m -> p c m", c=KB))
+        nc.sync.dma_start(x_t[:], x.rearrange("(p c) n -> p c n", c=KB))
+        nc.sync.dma_start(w_t[1][:], w[1].rearrange("(p c) m -> p c m", c=KB))
+        nc.scalar.dma_start(bias_t[:], b.rearrange("(m p) o -> p (m o)", p=P))
+        make_identity(nc, ident[:])
+
+        for m in range(MB):
+            nc.tensor.matmul(windows[m][:], ident[:], base_t[:, m, :], start=True, stop=False)
+
+        for e in range(E):
+            places = offs_t[:, e * (Q // 16) : (e + 1) * (Q // 16)]
+            for m in range(MB):
+                for c in range(KB):
+                    nc.tensor.matmul(
+                        windows[m][:].indirect(places),
+                        w_t[e][:, c, m * P : (m + 1) * P],
+                        x_t[:, c, e * Q : (e + 1) * Q],
+                        start=False,
+                        stop=(e == E - 1 and c == KB - 1),
+                    )
+
+        for m in range(MB):
+            out_t = held.tile([P, N], F32, name=f"out_t{m}")
+            nc.vector.tensor_scalar_add(out_t[:], windows[m][:], bias_t[:, m : m + 1])
+            nc.sync.dma_start(out[m * P : (m + 1) * P, :], out_t[:])

@@ -8,6 +8,7 @@ K, N = 512, 512
 M, E = 256, 2
 Q = N // E
 KB, MB = K // P, M // P
+WARM_UPS = 4
 
 FLOPS = 2 * K * N * M
 
@@ -21,18 +22,25 @@ def tile_scatter_matmul_kernel(tc, base, x, w, b, offs, out):
         ident = held.tile([P, P], BF16, name="ident")
         base_t = held.tile([P, MB, N], BF16, name="base_t")
         offs_t = held.tile([P, N // 16], U16, name="offs_t")
-        x_t = held.tile([P, KB, N], BF16, name="x_t")
+        x_t = [held.tile([P, KB, Q], BF16, name=f"x_t{e}") for e in range(E)]
         w_t = [held.tile([P, KB, M], BF16, name=f"w_t{e}") for e in range(E)]
         bias_t = held.tile([P, MB], F32, name="bias_t")
+        zeros = held.tile([P, N], BF16, name="zeros")
+        spare = psum.tile([P, N], F32, name="spare")
         windows = [psum.tile([P, N], F32, name=f"window{m}") for m in range(MB)]
 
         nc.sync.dma_start(base_t[:], base.rearrange("(m p) t -> p m t", p=P))
         nc.sync.dma_start(offs_t[:], offs)
-        nc.sync.dma_start(w_t[0][:], w[0].rearrange("(p c) m -> p c m", c=KB))
-        nc.sync.dma_start(x_t[:], x.rearrange("(p c) n -> p c n", c=KB))
-        nc.sync.dma_start(w_t[1][:], w[1].rearrange("(p c) m -> p c m", c=KB))
+        x_by_row = x.rearrange("(p c) n -> p c n", c=KB)
+        for e in range(E):
+            nc.sync.dma_start(w_t[e][:], w[e].rearrange("(p c) m -> p c m", c=KB))
+            nc.sync.dma_start(x_t[e][:], x_by_row[:, :, e * Q : (e + 1) * Q])
         nc.scalar.dma_start(bias_t[:], b.rearrange("(m p) o -> p (m o)", p=P))
         make_identity(nc, ident[:])
+
+        nc.vector.memset(zeros[:], 0.0)
+        for i in range(WARM_UPS):
+            nc.tensor.matmul(spare[:], zeros[:, :P], zeros[:], start=True, stop=True)
 
         for m in range(MB):
             nc.tensor.matmul(windows[m][:], ident[:], base_t[:, m, :], start=True, stop=False)
@@ -44,7 +52,7 @@ def tile_scatter_matmul_kernel(tc, base, x, w, b, offs, out):
                     nc.tensor.matmul(
                         windows[m][:].indirect(places),
                         w_t[e][:, c, m * P : (m + 1) * P],
-                        x_t[:, c, e * Q : (e + 1) * Q],
+                        x_t[e][:, c, :],
                         start=False,
                         stop=(e == E - 1 and c == KB - 1),
                     )

@@ -35,7 +35,7 @@ def tile_scatter_matmul_kernel(tc, base, x, w, b, offs, out):
         for e in range(E):
             nc.sync.dma_start(w_t[e][:], w[e].rearrange("(p c) m -> p c m", c=KB))
             nc.sync.dma_start(x_t[e][:], x_by_row[:, :, e * Q : (e + 1) * Q])
-        nc.scalar.dma_start(bias_t[:], b.rearrange("(m p) o -> p (m o)", p=P))
+        nc.sync.dma_start(bias_t[:], b.rearrange("(m p) o -> p (m o)", p=P))
         make_identity(nc, ident[:])
 
         nc.vector.memset(zeros[:], 0.0)

@@ -8,7 +8,7 @@ K, N = 512, 512
 M, E = 256, 2
 Q = N // E
 KB, MB = K // P, M // P
-WARM_UPS = 4
+WARM_UPS = 3
 
 FLOPS = 2 * K * N * M
 
@@ -22,8 +22,8 @@ def tile_scatter_matmul_kernel(tc, base, x, w, b, offs, out):
         ident = held.tile([P, P], BF16, name="ident")
         base_t = held.tile([P, MB, N], BF16, name="base_t")
         offs_t = held.tile([P, N // 16], U16, name="offs_t")
-        x_t = [held.tile([P, KB, Q], BF16, name=f"x_t{e}") for e in range(E)]
-        w_t = [held.tile([P, KB, M], BF16, name=f"w_t{e}") for e in range(E)]
+        x_t = [held.tile([P, N], BF16, name=f"x_t{c}") for c in range(KB)]
+        w_t = [held.tile([P, E, M], BF16, name=f"w_t{c}") for c in range(KB)]
         bias_t = held.tile([P, MB], F32, name="bias_t")
         zeros = held.tile([P, N], BF16, name="zeros")
         spare = psum.tile([P, N], F32, name="spare")
@@ -31,10 +31,9 @@ def tile_scatter_matmul_kernel(tc, base, x, w, b, offs, out):
 
         nc.sync.dma_start(base_t[:], base.rearrange("(m p) t -> p m t", p=P))
         nc.sync.dma_start(offs_t[:], offs)
-        x_by_row = x.rearrange("(p c) n -> p c n", c=KB)
-        for e in range(E):
-            nc.sync.dma_start(w_t[e][:], w[e].rearrange("(p c) m -> p c m", c=KB))
-            nc.sync.dma_start(x_t[e][:], x_by_row[:, :, e * Q : (e + 1) * Q])
+        for c in range(KB):
+            nc.sync.dma_start(w_t[c][:], w[:, c * P : (c + 1) * P, :].rearrange("e p m -> p e m"))
+            nc.sync.dma_start(x_t[c][:], x[c * P : (c + 1) * P, :])
         nc.sync.dma_start(bias_t[:], b.rearrange("(m p) o -> p (m o)", p=P))
         make_identity(nc, ident[:])
 
@@ -45,19 +44,21 @@ def tile_scatter_matmul_kernel(tc, base, x, w, b, offs, out):
         for m in range(MB):
             nc.tensor.matmul(windows[m][:], ident[:], base_t[:, m, :], start=True, stop=False)
 
-        for e in range(E):
-            places = offs_t[:, e * (Q // 16) : (e + 1) * (Q // 16)]
+        for c in range(KB):
             for m in range(MB):
-                for c in range(KB):
+                for e in range(E):
                     nc.tensor.matmul(
-                        windows[m][:].indirect(places),
-                        w_t[e][:, c, m * P : (m + 1) * P],
-                        x_t[e][:, c, :],
+                        windows[m][:].indirect(offs_t[:, e * (Q // 16) : (e + 1) * (Q // 16)]),
+                        w_t[c][:, e, m * P : (m + 1) * P],
+                        x_t[c][:, e * Q : (e + 1) * Q],
                         start=False,
-                        stop=(e == E - 1 and c == KB - 1),
+                        stop=(c == KB - 1 and e == E - 1),
                     )
 
+        half = N // 2
         for m in range(MB):
-            out_t = held.tile([P, N], F32, name=f"out_t{m}")
-            nc.vector.tensor_scalar_add(out_t[:], windows[m][:], bias_t[:, m : m + 1])
-            nc.sync.dma_start(out[m * P : (m + 1) * P, :], out_t[:])
+            for h in range(2):
+                cols = slice(h * half, (h + 1) * half)
+                out_t = held.tile([P, half], F32, name=f"out_t{m}_{h}")
+                nc.vector.tensor_scalar_add(out_t[:], windows[m][:, cols], bias_t[:, m : m + 1])
+                nc.sync.dma_start(out[m * P : (m + 1) * P, cols], out_t[:])

import concourse.mybir as mybir
from concourse.masks import make_identity

BF16, F32, U16 = mybir.dt.bfloat16, mybir.dt.float32, mybir.dt.uint16

P = 128
K, N = 512, 512
M, E = 256, 2
Q = N // E
KB, MB = K // P, M // P
WARM_UPS = 3

FLOPS = 2 * K * N * M


def tile_scatter_matmul_kernel(tc, base, x, w, b, offs, out):
    nc = tc.nc
    with (
        tc.tile_pool(name="held", bufs=1) as held,
        tc.psum_pool(name="psum", bufs=1) as psum,
    ):
        ident = held.tile([P, P], BF16, name="ident")
        base_t = held.tile([P, MB, N], BF16, name="base_t")
        offs_t = held.tile([P, N // 16], U16, name="offs_t")
        x_t = [held.tile([P, N], BF16, name=f"x_t{c}") for c in range(KB)]
        w_t = [held.tile([P, E, M], BF16, name=f"w_t{c}") for c in range(KB)]
        bias_t = held.tile([P, MB], F32, name="bias_t")
        zeros = held.tile([P, N], BF16, name="zeros")
        spare = psum.tile([P, N], F32, name="spare")
        windows = [psum.tile([P, N], F32, name=f"window{m}") for m in range(MB)]

        nc.sync.dma_start(base_t[:], base.rearrange("(m p) t -> p m t", p=P))
        nc.sync.dma_start(offs_t[:], offs)
        for c in range(KB):
            nc.sync.dma_start(w_t[c][:], w[:, c * P : (c + 1) * P, :].rearrange("e p m -> p e m"))
            nc.sync.dma_start(x_t[c][:], x[c * P : (c + 1) * P, :])
        nc.sync.dma_start(bias_t[:], b.rearrange("(m p) o -> p (m o)", p=P))
        make_identity(nc, ident[:])

        nc.vector.memset(zeros[:], 0.0)
        for i in range(WARM_UPS):
            nc.tensor.matmul(spare[:], zeros[:, :P], zeros[:], start=True, stop=True)

        for m in range(MB):
            nc.tensor.matmul(windows[m][:], ident[:], base_t[:, m, :], start=True, stop=False)

        for c in range(KB):
            for m in range(MB):
                for e in range(E):
                    nc.tensor.matmul(
                        windows[m][:].indirect(offs_t[:, e * (Q // 16) : (e + 1) * (Q // 16)]),
                        w_t[c][:, e, m * P : (m + 1) * P],
                        x_t[c][:, e * Q : (e + 1) * Q],
                        start=False,
                        stop=(c == KB - 1 and e == E - 1),
                    )

        half = N // 2
        for m in range(MB):
            for h in range(2):
                cols = slice(h * half, (h + 1) * half)
                out_t = held.tile([P, half], F32, name=f"out_t{m}_{h}")
                nc.vector.tensor_scalar_add(out_t[:], windows[m][:, cols], bias_t[:, m : m + 1])
                nc.sync.dma_start(out[m * P : (m + 1) * P, cols], out_t[:])
